import numpy as np
import ml_dtypes


def mxq(x, axis, fmt="e4m3"):
    dtype, down = {"e4m3": (ml_dtypes.float8_e4m3fn, 7), "e5m2": (ml_dtypes.float8_e5m2, 14)}[fmt]
    v = np.moveaxis(np.asarray(x, np.float32).astype(ml_dtypes.bfloat16).astype(np.float64), axis, -1)
    blocks = v.reshape(v.shape[:-1] + (-1, 32))
    amax = np.abs(blocks).max(-1, keepdims=True)
    byte = np.maximum(np.where(amax > 0, np.frexp(amax)[1] - 1 + 127, 0) - down, 1)
    scale = np.exp2(byte - 127.0)
    codes = (blocks / scale).astype(np.float32).astype(dtype).astype(np.float64)
    return np.moveaxis((codes * scale).reshape(v.shape), -1, axis)


WIDE = False


def mx_kscale(k):
    if not WIDE:
        return np.ones(k)
    levels = np.array([10, -10, 5, -5, 0])
    if k % 512:
        return np.exp2(np.random.permutation(np.resize(levels, k // 32))).repeat(32)
    a = np.empty((k // 512, 16))
    for p in range(k // 512):
        a[p, :8] = np.random.permutation(np.resize(levels, 8))
        for g in range(8):
            far = levels[np.abs(levels - a[p, g]) >= 10]
            a[p, g + 8] = far[np.random.randint(len(far))]
    return np.exp2(a.ravel()).repeat(32)


def f64(x):
    return np.asarray(x).astype(np.float64)


def striped8(idx):
    return np.asarray(idx).reshape(8, -1, 16).transpose(0, 2, 1).reshape(128, -1).astype(np.uint16)


def unstriped8(offs):
    return offs.reshape(8, 16, -1).transpose(0, 2, 1).reshape(8, -1).astype(np.int64)


def pick8(x, idx, run):
    r = np.arange(len(x))
    return x[r[:, None], idx[r % (8 * run) // run]]


E2M1 = np.array([0.0, 0.5, 1.0, 1.5, 2.0, 3.0, 4.0, 6.0, -0.0, -0.5, -1.0, -1.5, -2.0, -3.0, -4.0, -6.0])


def pack_weight(w, fmt):
    k, n = w.shape
    w = f64(np.asarray(w, np.float32).astype(ml_dtypes.bfloat16)).reshape(k // 32, 32, n)
    amax = np.abs(w).max(1)
    if fmt == "e4m3":
        byte = np.frexp(amax)[1] - 1 + 127 - 7
    else:
        mant, ex = np.frexp(amax / 6.0)
        byte = np.where(mant > 0.5, ex, ex - 1) + 127
    byte = np.clip(np.where(amax > 0, byte, 1), 1, 254)
    scaled = (w * np.exp2(127.0 - byte)[:, None, :]).reshape(k, n).astype(np.float32)
    by_word = np.ascontiguousarray(scaled.reshape(k // 512, 128, 4, n).transpose(0, 1, 3, 2))
    if fmt == "e4m3":
        words = by_word.astype(ml_dtypes.float8_e4m3fn).view(np.uint8)
    else:
        c = by_word.astype(ml_dtypes.float4_e2m1fn).view(np.uint8) & 0xF
        words = (c[..., 0::2] | (c[..., 1::2] << 4)).reshape(k // 512, 128, 2 * n)
    return np.ascontiguousarray(words), np.ascontiguousarray(byte.astype(np.uint8).reshape(k // 512, 16, n))


def unpack_weight(words, scales, fmt):
    g, _, n = scales.shape
    words = np.ascontiguousarray(words).reshape(g, 128, n, -1)
    if fmt == "e4m3":
        vals = words.view(ml_dtypes.float8_e4m3fn).astype(np.float64)
    else:
        nib = np.empty((g, 128, n, 4), np.uint8)
        nib[..., 0::2] = words & 0xF
        nib[..., 1::2] = words >> 4
        vals = E2M1[nib]
    vals = vals * np.repeat(np.exp2(scales.astype(np.float64) - 127.0), 8, axis=1)[..., None]
    return vals.transpose(0, 1, 3, 2).reshape(g * 512, n)


D, T, I, Q = 512, 1024, 512, 128


def setup_inputs():
    n = np.random.standard_normal
    idx = np.stack([np.random.permutation(T)[:I] for _ in range(8)])
    idx2 = np.stack([np.random.permutation(T)[:I] for _ in range(8)])
    idx3 = np.stack([np.random.permutation(T)[:I] for _ in range(8)])
    idx4 = np.stack([np.random.permutation(T)[:I] for _ in range(8)])
    fd = mx_kscale(D)
    keysp = pack_weight(n((D, T)) / fd[:, None], "e4m3")
    return {
        "query": (n((D, Q)) * 0.9 / np.sqrt(D) * fd[:, None]).astype(np.float32),
        "keys_words": keysp[0],
        "keys_scales": keysp[1],
        "lam": (np.random.uniform(0.3, 0.9, (Q, 1))).astype(np.float32),
        "old": (1.0 * n((Q, T))).astype(np.float32),
        "offs": striped8(idx),
        "offs2": striped8(idx2),
        "offs3": striped8(idx3),
        "offs4": striped8(idx4),
    }


def reference(query, keys_words, keys_scales, lam, old, offs, offs2, offs3, offs4):
    idx = unstriped8(offs)
    idx2 = unstriped8(offs2)
    idx3 = unstriped8(offs3)
    idx4 = unstriped8(offs4)
    keysu = unpack_weight(keys_words, keys_scales, "e4m3")
    queryq = mxq(f64(query), 0, "e4m3")
    a = queryq.T @ keysu
    w = pick8(a, idx, 16) + np.maximum(pick8(a, idx2, 16), pick8(a, idx3, 16)) * f64(lam)
    f1 = np.zeros((Q, T))
    f1[np.arange(Q)[:, None], idx4[np.arange(Q) % 128 // 16]] = w
    y = np.maximum(f1, f64(old)) + f64(old) * 0.25
    return y

@@ -1,0 +1,137 @@
+from contextlib import ExitStack
+
+import concourse.mybir as mybir
+
+D, T, SLOTS, Q = 512, 1024, 512, 128
+FLOPS = 2 * D * Q * T
+
+F32 = mybir.dt.float32
+BF16 = mybir.dt.bfloat16
+I32 = mybir.dt.int32
+U32 = mybir.dt.uint32
+U16 = mybir.dt.uint16
+U8 = mybir.dt.uint8
+FP8X4 = mybir.dt.float8_e4m3fn_x4
+ALU = mybir.AluOpType
+COPY = mybir.ActivationFunctionType.Copy
+
+P = 128
+PACK = 4
+N_PASS = 256
+PASSES = T // N_PASS
+KEY_LOAD = 512
+HALF = SLOTS // 2
+LIST_COLS = HALF // 16
+OUT_WIDTHS = (256, 256, 256, 128, 128)
+
+
+def tile_attend_lookahead_lean_largerput_heads_kernel(tc, query, keys_words, keys_scales, lam, old, offs, offs2, offs3, offs4, out):
+    nc = tc.nc
+    with ExitStack() as ctx:
+        pool = ctx.enter_context(tc.tile_pool(name="pool", bufs=1))
+        psum = ctx.enter_context(tc.psum_pool(name="psum", bufs=1))
+
+        key_scales = pool.tile([P, N_PASS], U8, align_bytes=64)
+        nc.vector.memset(key_scales[:].bitcast(I32), 0)
+
+        q_raw = pool.tile([P, PACK, Q], F32)
+        nc.sync.dma_start(out=q_raw[:], in_=query.rearrange("(p j) q -> p j q", j=PACK))
+
+        for quad in range(4):
+            rows = keys_scales[0, 4 * quad : 4 * quad + 4, :].bitcast(I32)
+            nc.scalar.dma_start(
+                out=key_scales[32 * quad : 32 * quad + 16, :].bitcast(I32),
+                in_=rows.rearrange("r (j n) -> j r n", j=PASSES),
+            )
+
+        words = keys_words[0].rearrange("p n t -> p (n t)").bitcast(I32)
+        key_words = []
+        for u in range(T // KEY_LOAD):
+            part = pool.tile([P, KEY_LOAD], U32, align_bytes=64, name="key_words%d" % u)
+            nc.sync.dma_start(out=part[:].bitcast(I32), in_=words[:, u * KEY_LOAD : (u + 1) * KEY_LOAD])
+            key_words.append(part)
+
+        list3 = pool.tile([P, SLOTS // 16], U16)
+        nc.sync.dma_start(list3[:], offs3)
+        list2 = pool.tile([P, SLOTS // 16], U16)
+        nc.sync.dma_start(list2[:], offs2)
+        list1 = pool.tile([P, SLOTS // 16], U16)
+        nc.sync.dma_start(list1[:], offs)
+        lam_sb = pool.tile([P, 1], F32)
+        nc.sync.dma_start(out=lam_sb[:], in_=lam)
+        list4 = pool.tile([P, SLOTS // 16], U16)
+        nc.sync.dma_start(list4[:], offs4)
+        old_sb = pool.tile([P, T], F32)
+        nc.sync.dma_start(out=old_sb[:], in_=old)
+
+        placed = pool.tile([P, T], F32)
+        nc.vector.memset(placed[:], 0.0)
+
+        q_grouped = pool.tile([P, Q, PACK], BF16, align_bytes=64)
+        nc.vector.tensor_copy(
+            out=q_grouped[:].rearrange("p (c i) j -> p c j i", i=4),
+            in_=q_raw[:].rearrange("p j (c i) -> p c j i", i=4),
+        )
+        q_codes = pool.tile([P, Q], U32, align_bytes=64)
+        q_scales = pool.tile([P, Q], U8, align_bytes=64)
+        nc.vector.quantize_mx(
+            out=q_codes[:].bitcast(FP8X4), scales=q_scales[:], in_=q_grouped[:].rearrange("p q j -> p (q j)")
+        )
+
+        scores = pool.tile([P, T], F32)
+        for j in range(PASSES):
+            bank = psum.tile([P, N_PASS], F32, name="bank%d" % j)
+            part, first = divmod(j * N_PASS, KEY_LOAD)
+            nc.tensor.matmul_mx(
+                out=bank[:],
+                lhsT=q_codes[:].bitcast(FP8X4),
+                lhsT_scale=q_scales[:],
+                rhs=key_words[part][:, first : first + N_PASS].bitcast(FP8X4),
+                rhs_scale=key_scales[4 * j : P, :],
+                start=True,
+                stop=True,
+            )
+            cols = slice(j * N_PASS, (j + 1) * N_PASS)
+            if j % 2 == 0:
+                nc.scalar.copy(out=scores[:, cols], in_=bank[:])
+            else:
+                nc.vector.tensor_copy(out=scores[:, cols], in_=bank[:])
+
+        halves = range(2)
+        lists = [slice(h * LIST_COLS, (h + 1) * LIST_COLS) for h in halves]
+        follower2 = [pool.tile([P, HALF], F32, name="follower2_%d" % h) for h in halves]
+        follower3 = [pool.tile([P, HALF], F32, name="follower3_%d" % h) for h in halves]
+        token = [pool.tile([P, HALF], F32, name="token_%d" % h) for h in halves]
+        larger = [pool.tile([P, HALF], F32, name="larger_%d" % h) for h in halves]
+        leaned = [pool.tile([P, HALF], F32, name="leaned_%d" % h) for h in halves]
+        for h in halves:
+            nc.vector.tensor_copy(follower3[h][:], scores[:].indirect(list3[:, lists[h]]))
+            nc.scalar.activation(follower2[h][:], scores[:].indirect(list2[:, lists[h]]), COPY)
+        for h in halves:
+            nc.scalar.activation(token[h][:], scores[:].indirect(list1[:, lists[h]]), COPY)
+        for h in halves:
+            nc.vector.tensor_tensor(larger[h][:], follower2[h][:], follower3[h][:], ALU.max)
+        for h in halves:
+            nc.vector.tensor_scalar(leaned[h][:], larger[h][:], lam_sb[:, 0:1], None, ALU.mult)
+        for h in halves:
+            nc.vector.tensor_tensor(placed[:].indirect(list4[:, lists[h]]), token[h][:], leaned[h][:], ALU.add)
+
+        starts = [sum(OUT_WIDTHS[:c]) for c in range(len(OUT_WIDTHS))]
+        kept = [pool.tile([P, w], F32, name="kept%d" % c) for c, w in enumerate(OUT_WIDTHS)]
+        result = [pool.tile([P, w], F32, name="result%d" % c) for c, w in enumerate(OUT_WIDTHS)]
+
+        def keep_larger(c):
+            cols = slice(starts[c], starts[c] + OUT_WIDTHS[c])
+            nc.vector.tensor_tensor(kept[c][:], placed[:, cols], old_sb[:, cols], ALU.max)
+
+        def add_quarter_and_store(c):
+            cols = slice(starts[c], starts[c] + OUT_WIDTHS[c])
+            nc.vector.scalar_tensor_tensor(result[c][:], old_sb[:, cols], 0.25, kept[c][:], ALU.mult, ALU.add)
+            queue = nc.sync if c % 2 == 0 else nc.scalar
+            queue.dma_start(out=out[:, cols], in_=result[c][:])
+
+        keep_larger(0)
+        for c in range(1, len(OUT_WIDTHS)):
+            keep_larger(c)
+            add_quarter_and_store(c - 1)
+        add_quarter_and_store(len(OUT_WIDTHS) - 1)

@@ -1,6 +1,7 @@
 from contextlib import ExitStack
 
 import concourse.mybir as mybir
+from concourse.masks import make_identity
 
 D, T, SLOTS, Q = 512, 1024, 512, 128
 FLOPS = 2 * D * Q * T
@@ -22,7 +23,11 @@ PASSES = T // N_PASS
 KEY_LOAD = 512
 HALF = SLOTS // 2
 LIST_COLS = HALF // 16
-OUT_WIDTHS = (256, 256, 256, 128, 128)
+PASS_WIDTHS = (256, 256, 256, 128, 128)
+Q_VECTOR = 88
+BANK = 512
+OWN_WIDTHS = (128, 128, 256)
+SHARED_WIDTHS = (320, 192)
 
 
 def tile_attend_lookahead_lean_largerput_heads_kernel(tc, query, keys_words, keys_scales, lam, old, offs, offs2, offs3, offs4, out):
@@ -39,7 +44,7 @@ def tile_attend_lookahead_lean_largerput_heads_kernel(tc, query, keys_words, key
 
         for quad in range(4):
             rows = keys_scales[0, 4 * quad : 4 * quad + 4, :].bitcast(I32)
-            nc.scalar.dma_start(
+            nc.sync.dma_start(
                 out=key_scales[32 * quad : 32 * quad + 16, :].bitcast(I32),
                 in_=rows.rearrange("r (j n) -> j r n", j=PASSES),
             )
@@ -68,34 +73,34 @@ def tile_attend_lookahead_lean_largerput_heads_kernel(tc, query, keys_words, key
         nc.vector.memset(placed[:], 0.0)
 
         q_grouped = pool.tile([P, Q, PACK], BF16, align_bytes=64)
-        nc.vector.tensor_copy(
-            out=q_grouped[:].rearrange("p (c i) j -> p c j i", i=4),
-            in_=q_raw[:].rearrange("p j (c i) -> p c j i", i=4),
-        )
+        for copy, cols in ((nc.vector.tensor_copy, slice(0, Q_VECTOR)), (nc.scalar.copy, slice(Q_VECTOR, Q))):
+            copy(
+                out=q_grouped[:, cols, :].rearrange("p (c i) j -> p c j i", i=4),
+                in_=q_raw[:, :, cols].rearrange("p j (c i) -> p c j i", i=4),
+            )
         q_codes = pool.tile([P, Q], U32, align_bytes=64)
         q_scales = pool.tile([P, Q], U8, align_bytes=64)
         nc.vector.quantize_mx(
             out=q_codes[:].bitcast(FP8X4), scales=q_scales[:], in_=q_grouped[:].rearrange("p q j -> p (q j)")
         )
 
-        scores = pool.tile([P, T], F32)
-        for j in range(PASSES):
-            bank = psum.tile([P, N_PASS], F32, name="bank%d" % j)
-            part, first = divmod(j * N_PASS, KEY_LOAD)
+        scores = pool.tile([P, T], F32, tag="wide")
+        for j, width in enumerate(PASS_WIDTHS):
+            start = sum(PASS_WIDTHS[:j])
+            bank = psum.tile([P, width], F32, name="bank%d" % j)
+            part, first = divmod(start, KEY_LOAD)
+            plane, column = divmod(start, N_PASS)
             nc.tensor.matmul_mx(
                 out=bank[:],
                 lhsT=q_codes[:].bitcast(FP8X4),
                 lhsT_scale=q_scales[:],
-                rhs=key_words[part][:, first : first + N_PASS].bitcast(FP8X4),
-                rhs_scale=key_scales[4 * j : P, :],
+                rhs=key_words[part][:, first : first + width].bitcast(FP8X4),
+                rhs_scale=key_scales[4 * plane : P, column : column + width],
                 start=True,
                 stop=True,
             )
-            cols = slice(j * N_PASS, (j + 1) * N_PASS)
-            if j % 2 == 0:
-                nc.scalar.copy(out=scores[:, cols], in_=bank[:])
-            else:
-                nc.vector.tensor_copy(out=scores[:, cols], in_=bank[:])
+            copy = nc.vector.tensor_copy if j % 2 == 0 else nc.scalar.copy
+            copy(out=scores[:, start : start + width], in_=bank[:])
 
         halves = range(2)
         lists = [slice(h * LIST_COLS, (h + 1) * LIST_COLS) for h in halves]
@@ -116,22 +121,51 @@ def tile_attend_lookahead_lean_largerput_heads_kernel(tc, query, keys_words, key
         for h in halves:
             nc.vector.tensor_tensor(placed[:].indirect(list4[:, lists[h]]), token[h][:], leaned[h][:], ALU.add)
 
-        starts = [sum(OUT_WIDTHS[:c]) for c in range(len(OUT_WIDTHS))]
-        kept = [pool.tile([P, w], F32, name="kept%d" % c) for c, w in enumerate(OUT_WIDTHS)]
-        result = [pool.tile([P, w], F32, name="result%d" % c) for c, w in enumerate(OUT_WIDTHS)]
+        identity = pool.tile([P, P], F32)
+        make_identity(nc, identity[:])
+        old_turned = pool.tile([P, T], F32, tag="wide")
+        old_psum = []
+        for u, factor in enumerate((1.0, 1.25)):
+            turned = psum.tile([P, BANK], F32, name="turned%d" % u, tag="bank%d" % u)
+            for blk in range(0, BANK, P):
+                nc.tensor.transpose(turned[:, blk : blk + P], old_sb[:, u * BANK + blk : u * BANK + blk + P], identity[:])
+            nc.scalar.activation(old_turned[:, u * BANK : (u + 1) * BANK], turned[:], COPY, scale=factor)
+            back = psum.tile([P, BANK], F32, name="back%d" % u)
+            for blk in range(0, BANK, P):
+                nc.tensor.transpose(back[:, blk : blk + P], old_turned[:, u * BANK + blk : u * BANK + blk + P], identity[:])
+            old_psum.append(back)
+
+        own = [slice(sum(OWN_WIDTHS[:c]), sum(OWN_WIDTHS[: c + 1])) for c in range(len(OWN_WIDTHS))]
+        shared = [slice(sum(SHARED_WIDTHS[:c]), sum(SHARED_WIDTHS[: c + 1])) for c in range(len(SHARED_WIDTHS))]
+        kept = [pool.tile([P, w], F32, name="kept%d" % c) for c, w in enumerate(OWN_WIDTHS)]
+        own_result = [pool.tile([P, w], F32, name="own_result%d" % c) for c, w in enumerate(OWN_WIDTHS)]
+        excess = [pool.tile([P, w], F32, name="excess%d" % c) for c, w in enumerate(SHARED_WIDTHS)]
+        shared_result = [pool.tile([P, w], F32, name="shared_result%d" % c) for c, w in enumerate(SHARED_WIDTHS)]
+
+        for c, cols in enumerate(shared):
+            wide = slice(BANK + cols.start, BANK + cols.stop)
+            nc.gpsimd.tensor_tensor(excess[c][:], placed[:, wide], old_sb[:, wide], ALU.subtract)
 
         def keep_larger(c):
-            cols = slice(starts[c], starts[c] + OUT_WIDTHS[c])
-            nc.vector.tensor_tensor(kept[c][:], placed[:, cols], old_sb[:, cols], ALU.max)
+            nc.vector.tensor_tensor(kept[c][:], placed[:, own[c]], old_psum[0][:, own[c]], ALU.max)
 
-        def add_quarter_and_store(c):
-            cols = slice(starts[c], starts[c] + OUT_WIDTHS[c])
-            nc.vector.scalar_tensor_tensor(result[c][:], old_sb[:, cols], 0.25, kept[c][:], ALU.mult, ALU.add)
-            queue = nc.sync if c % 2 == 0 else nc.scalar
-            queue.dma_start(out=out[:, cols], in_=result[c][:])
+        def add_quarter(c, queue):
+            nc.vector.scalar_tensor_tensor(
+                own_result[c][:], old_psum[0][:, own[c]], 0.25, kept[c][:], ALU.mult, ALU.add
+            )
+            queue.dma_start(out=out[:, own[c]], in_=own_result[c][:])
+
+        def finish_shared(c, queue):
+            nc.vector.scalar_tensor_tensor(
+                shared_result[c][:], excess[c][:], 0.0, old_psum[1][:, shared[c]], ALU.max, ALU.add
+            )
+            queue.dma_start(out=out[:, BANK + shared[c].start : BANK + shared[c].stop], in_=shared_result[c][:])
 
         keep_larger(0)
-        for c in range(1, len(OUT_WIDTHS)):
-            keep_larger(c)
-            add_quarter_and_store(c - 1)
-        add_quarter_and_store(len(OUT_WIDTHS) - 1)
+        keep_larger(1)
+        add_quarter(0, nc.sync)
+        keep_larger(2)
+        add_quarter(1, nc.scalar)
+        add_quarter(2, nc.sync)
+        finish_shared(0, nc.scalar)
+        finish_shared(1, nc.sync)

@@ -42,19 +42,16 @@ def tile_attend_lookahead_lean_largerput_heads_kernel(tc, query, keys_words, key
         q_raw = pool.tile([P, PACK, Q], F32)
         nc.sync.dma_start(out=q_raw[:], in_=query.rearrange("(p j) q -> p j q", j=PACK))
 
+        words = keys_words[0].rearrange("p n t -> p (n t)").bitcast(I32)
+        key_words = [pool.tile([P, KEY_LOAD], U32, align_bytes=64, name="key_words%d" % u) for u in range(2)]
+        nc.sync.dma_start(out=key_words[0][:].bitcast(I32), in_=words[:, 0:KEY_LOAD])
         for quad in range(4):
             rows = keys_scales[0, 4 * quad : 4 * quad + 4, :].bitcast(I32)
             nc.sync.dma_start(
                 out=key_scales[32 * quad : 32 * quad + 16, :].bitcast(I32),
                 in_=rows.rearrange("r (j n) -> j r n", j=PASSES),
             )
-
-        words = keys_words[0].rearrange("p n t -> p (n t)").bitcast(I32)
-        key_words = []
-        for u in range(T // KEY_LOAD):
-            part = pool.tile([P, KEY_LOAD], U32, align_bytes=64, name="key_words%d" % u)
-            nc.sync.dma_start(out=part[:].bitcast(I32), in_=words[:, u * KEY_LOAD : (u + 1) * KEY_LOAD])
-            key_words.append(part)
+        nc.sync.dma_start(out=key_words[1][:].bitcast(I32), in_=words[:, KEY_LOAD:T])
 
         list3 = pool.tile([P, SLOTS // 16], U16)
         nc.sync.dma_start(list3[:], offs3)
@@ -72,7 +69,7 @@ def tile_attend_lookahead_lean_largerput_heads_kernel(tc, query, keys_words, key
         placed = pool.tile([P, T], F32)
         nc.vector.memset(placed[:], 0.0)
 
-        q_grouped = pool.tile([P, Q, PACK], BF16, align_bytes=64)
+        q_grouped = pool.tile([P, Q, PACK], BF16, align_bytes=64, tag="early")
         for copy, cols in ((nc.vector.tensor_copy, slice(0, Q_VECTOR)), (nc.scalar.copy, slice(Q_VECTOR, Q))):
             copy(
                 out=q_grouped[:, cols, :].rearrange("p (c i) j -> p c j i", i=4),
@@ -121,7 +118,7 @@ def tile_attend_lookahead_lean_largerput_heads_kernel(tc, query, keys_words, key
         for h in halves:
             nc.vector.tensor_tensor(placed[:].indirect(list4[:, lists[h]]), token[h][:], leaned[h][:], ALU.add)
 
-        identity = pool.tile([P, P], F32)
+        identity = pool.tile([P, P], F32, align_bytes=64, tag="early")
         make_identity(nc, identity[:])
         old_turned = pool.tile([P, T], F32, tag="wide")
         old_psum = []

@@ -20,10 +20,10 @@ P = 128
 PACK = 4
 N_PASS = 256
 PASSES = T // N_PASS
-KEY_LOAD = 512
+KEY_LOADS = (384, 384, 256)
 HALF = SLOTS // 2
 LIST_COLS = HALF // 16
-PASS_WIDTHS = (256, 256, 256, 128, 128)
+PASS_WIDTHS = ((256, 128), (128, 256), (128, 128))
 Q_VECTOR = 88
 BANK = 512
 OWN_WIDTHS = (128, 128, 256)
@@ -43,15 +43,21 @@ def tile_attend_lookahead_lean_largerput_heads_kernel(tc, query, keys_words, key
         nc.sync.dma_start(out=q_raw[:], in_=query.rearrange("(p j) q -> p j q", j=PACK))
 
         words = keys_words[0].rearrange("p n t -> p (n t)").bitcast(I32)
-        key_words = [pool.tile([P, KEY_LOAD], U32, align_bytes=64, name="key_words%d" % u) for u in range(2)]
-        nc.sync.dma_start(out=key_words[0][:].bitcast(I32), in_=words[:, 0:KEY_LOAD])
+        key_words = [pool.tile([P, w], U32, align_bytes=64, name="key_words%d" % u) for u, w in enumerate(KEY_LOADS)]
+
+        def load_keys(u):
+            first = sum(KEY_LOADS[:u])
+            nc.sync.dma_start(out=key_words[u][:].bitcast(I32), in_=words[:, first : first + KEY_LOADS[u]])
+
+        load_keys(0)
         for quad in range(4):
             rows = keys_scales[0, 4 * quad : 4 * quad + 4, :].bitcast(I32)
             nc.sync.dma_start(
                 out=key_scales[32 * quad : 32 * quad + 16, :].bitcast(I32),
                 in_=rows.rearrange("r (j n) -> j r n", j=PASSES),
             )
-        nc.sync.dma_start(out=key_words[1][:].bitcast(I32), in_=words[:, KEY_LOAD:T])
+        load_keys(1)
+        load_keys(2)
 
         list3 = pool.tile([P, SLOTS // 16], U16)
         nc.sync.dma_start(list3[:], offs3)
@@ -82,10 +88,10 @@ def tile_attend_lookahead_lean_largerput_heads_kernel(tc, query, keys_words, key
         )
 
         scores = pool.tile([P, T], F32, tag="wide")
-        for j, width in enumerate(PASS_WIDTHS):
-            start = sum(PASS_WIDTHS[:j])
+        passes = [(u, sum(ws[:i]), w) for u, ws in enumerate(PASS_WIDTHS) for i, w in enumerate(ws)]
+        for j, (part, first, width) in enumerate(passes):
+            start = sum(KEY_LOADS[:part]) + first
             bank = psum.tile([P, width], F32, name="bank%d" % j)
-            part, first = divmod(start, KEY_LOAD)
             plane, column = divmod(start, N_PASS)
             nc.tensor.matmul_mx(
                 out=bank[:],
@@ -96,7 +102,7 @@ def tile_attend_lookahead_lean_largerput_heads_kernel(tc, query, keys_words, key
                 start=True,
                 stop=True,
             )
-            copy = nc.vector.tensor_copy if j % 2 == 0 else nc.scalar.copy
+            copy = nc.vector.tensor_copy if j % 2 == 1 else nc.scalar.copy
             copy(out=scores[:, start : start + width], in_=bank[:])
 
         halves = range(2)

from contextlib import ExitStack

import concourse.mybir as mybir
from concourse.masks import make_identity

D, T, SLOTS, Q = 512, 1024, 512, 128
FLOPS = 2 * D * Q * T

F32 = mybir.dt.float32
BF16 = mybir.dt.bfloat16
I32 = mybir.dt.int32
U32 = mybir.dt.uint32
U16 = mybir.dt.uint16
U8 = mybir.dt.uint8
FP8X4 = mybir.dt.float8_e4m3fn_x4
ALU = mybir.AluOpType
COPY = mybir.ActivationFunctionType.Copy

P = 128
PACK = 4
N_PASS = 256
PASSES = T // N_PASS
KEY_LOADS = (384, 384, 256)
HALF = SLOTS // 2
LIST_COLS = HALF // 16
PASS_WIDTHS = ((256, 128), (128, 256), (128, 128))
Q_VECTOR = 88
BANK = 512
OWN_WIDTHS = (128, 128, 256)
SHARED_WIDTHS = (320, 192)


def tile_attend_lookahead_lean_largerput_heads_kernel(tc, query, keys_words, keys_scales, lam, old, offs, offs2, offs3, offs4, out):
    nc = tc.nc
    with ExitStack() as ctx:
        pool = ctx.enter_context(tc.tile_pool(name="pool", bufs=1))
        psum = ctx.enter_context(tc.psum_pool(name="psum", bufs=1))

        key_scales = pool.tile([P, N_PASS], U8, align_bytes=64)
        nc.vector.memset(key_scales[:].bitcast(I32), 0)

        q_raw = pool.tile([P, PACK, Q], F32)
        nc.sync.dma_start(out=q_raw[:], in_=query.rearrange("(p j) q -> p j q", j=PACK))

        words = keys_words[0].rearrange("p n t -> p (n t)").bitcast(I32)
        key_words = [pool.tile([P, w], U32, align_bytes=64, name="key_words%d" % u) for u, w in enumerate(KEY_LOADS)]

        def load_keys(u):
            first = sum(KEY_LOADS[:u])
            nc.sync.dma_start(out=key_words[u][:].bitcast(I32), in_=words[:, first : first + KEY_LOADS[u]])

        load_keys(0)
        for quad in range(4):
            rows = keys_scales[0, 4 * quad : 4 * quad + 4, :].bitcast(I32)
            nc.sync.dma_start(
                out=key_scales[32 * quad : 32 * quad + 16, :].bitcast(I32),
                in_=rows.rearrange("r (j n) -> j r n", j=PASSES),
            )
        load_keys(1)
        load_keys(2)

        list3 = pool.tile([P, SLOTS // 16], U16)
        nc.sync.dma_start(list3[:], offs3)
        list2 = pool.tile([P, SLOTS // 16], U16)
        nc.sync.dma_start(list2[:], offs2)
        list1 = pool.tile([P, SLOTS // 16], U16)
        nc.sync.dma_start(list1[:], offs)
        lam_sb = pool.tile([P, 1], F32)
        nc.sync.dma_start(out=lam_sb[:], in_=lam)
        list4 = pool.tile([P, SLOTS // 16], U16)
        nc.sync.dma_start(list4[:], offs4)
        old_sb = pool.tile([P, T], F32)
        nc.sync.dma_start(out=old_sb[:], in_=old)

        placed = pool.tile([P, T], F32)
        nc.vector.memset(placed[:], 0.0)

        q_grouped = pool.tile([P, Q, PACK], BF16, align_bytes=64, tag="early")
        for copy, cols in ((nc.vector.tensor_copy, slice(0, Q_VECTOR)), (nc.scalar.copy, slice(Q_VECTOR, Q))):
            copy(
                out=q_grouped[:, cols, :].rearrange("p (c i) j -> p c j i", i=4),
                in_=q_raw[:, :, cols].rearrange("p j (c i) -> p c j i", i=4),
            )
        q_codes = pool.tile([P, Q], U32, align_bytes=64)
        q_scales = pool.tile([P, Q], U8, align_bytes=64)
        nc.vector.quantize_mx(
            out=q_codes[:].bitcast(FP8X4), scales=q_scales[:], in_=q_grouped[:].rearrange("p q j -> p (q j)")
        )

        scores = pool.tile([P, T], F32, tag="wide")
        passes = [(u, sum(ws[:i]), w) for u, ws in enumerate(PASS_WIDTHS) for i, w in enumerate(ws)]
        for j, (part, first, width) in enumerate(passes):
            start = sum(KEY_LOADS[:part]) + first
            bank = psum.tile([P, width], F32, name="bank%d" % j)
            plane, column = divmod(start, N_PASS)
            nc.tensor.matmul_mx(
                out=bank[:],
                lhsT=q_codes[:].bitcast(FP8X4),
                lhsT_scale=q_scales[:],
                rhs=key_words[part][:, first : first + width].bitcast(FP8X4),
                rhs_scale=key_scales[4 * plane : P, column : column + width],
                start=True,
                stop=True,
            )
            copy = nc.vector.tensor_copy if j % 2 == 1 else nc.scalar.copy
            copy(out=scores[:, start : start + width], in_=bank[:])

        halves = range(2)
        lists = [slice(h * LIST_COLS, (h + 1) * LIST_COLS) for h in halves]
        follower2 = [pool.tile([P, HALF], F32, name="follower2_%d" % h) for h in halves]
        follower3 = [pool.tile([P, HALF], F32, name="follower3_%d" % h) for h in halves]
        token = [pool.tile([P, HALF], F32, name="token_%d" % h) for h in halves]
        larger = [pool.tile([P, HALF], F32, name="larger_%d" % h) for h in halves]
        leaned = [pool.tile([P, HALF], F32, name="leaned_%d" % h) for h in halves]
        for h in halves:
            nc.vector.tensor_copy(follower3[h][:], scores[:].indirect(list3[:, lists[h]]))
            nc.scalar.activation(follower2[h][:], scores[:].indirect(list2[:, lists[h]]), COPY)
        for h in halves:
            nc.scalar.activation(token[h][:], scores[:].indirect(list1[:, lists[h]]), COPY)
        for h in halves:
            nc.vector.tensor_tensor(larger[h][:], follower2[h][:], follower3[h][:], ALU.max)
        for h in halves:
            nc.vector.tensor_scalar(leaned[h][:], larger[h][:], lam_sb[:, 0:1], None, ALU.mult)
        for h in halves:
            nc.vector.tensor_tensor(placed[:].indirect(list4[:, lists[h]]), token[h][:], leaned[h][:], ALU.add)

        identity = pool.tile([P, P], F32, align_bytes=64, tag="early")
        make_identity(nc, identity[:])
        old_turned = pool.tile([P, T], F32, tag="wide")
        old_psum = []
        for u, factor in enumerate((1.0, 1.25)):
            turned = psum.tile([P, BANK], F32, name="turned%d" % u, tag="bank%d" % u)
            for blk in range(0, BANK, P):
                nc.tensor.transpose(turned[:, blk : blk + P], old_sb[:, u * BANK + blk : u * BANK + blk + P], identity[:])
            nc.scalar.activation(old_turned[:, u * BANK : (u + 1) * BANK], turned[:], COPY, scale=factor)
            back = psum.tile([P, BANK], F32, name="back%d" % u)
            for blk in range(0, BANK, P):
                nc.tensor.transpose(back[:, blk : blk + P], old_turned[:, u * BANK + blk : u * BANK + blk + P], identity[:])
            old_psum.append(back)

        own = [slice(sum(OWN_WIDTHS[:c]), sum(OWN_WIDTHS[: c + 1])) for c in range(len(OWN_WIDTHS))]
        shared = [slice(sum(SHARED_WIDTHS[:c]), sum(SHARED_WIDTHS[: c + 1])) for c in range(len(SHARED_WIDTHS))]
        kept = [pool.tile([P, w], F32, name="kept%d" % c) for c, w in enumerate(OWN_WIDTHS)]
        own_result = [pool.tile([P, w], F32, name="own_result%d" % c) for c, w in enumerate(OWN_WIDTHS)]
        excess = [pool.tile([P, w], F32, name="excess%d" % c) for c, w in enumerate(SHARED_WIDTHS)]
        shared_result = [pool.tile([P, w], F32, name="shared_result%d" % c) for c, w in enumerate(SHARED_WIDTHS)]

        for c, cols in enumerate(shared):
            wide = slice(BANK + cols.start, BANK + cols.stop)
            nc.gpsimd.tensor_tensor(excess[c][:], placed[:, wide], old_sb[:, wide], ALU.subtract)

        def keep_larger(c):
            nc.vector.tensor_tensor(kept[c][:], placed[:, own[c]], old_psum[0][:, own[c]], ALU.max)

        def add_quarter(c, queue):
            nc.vector.scalar_tensor_tensor(
                own_result[c][:], old_psum[0][:, own[c]], 0.25, kept[c][:], ALU.mult, ALU.add
            )
            queue.dma_start(out=out[:, own[c]], in_=own_result[c][:])

        def finish_shared(c, queue):
            nc.vector.scalar_tensor_tensor(
                shared_result[c][:], excess[c][:], 0.0, old_psum[1][:, shared[c]], ALU.max, ALU.add
            )
            queue.dma_start(out=out[:, BANK + shared[c].start : BANK + shared[c].stop], in_=shared_result[c][:])

        keep_larger(0)
        keep_larger(1)
        add_quarter(0, nc.sync)
        keep_larger(2)
        add_quarter(1, nc.scalar)
        add_quarter(2, nc.sync)
        finish_shared(0, nc.scalar)
        finish_shared(1, nc.sync)
